import numpy as np
import ml_dtypes


def mxq(x, axis, fmt="e4m3"):
    dtype, down = {"e4m3": (ml_dtypes.float8_e4m3fn, 7), "e5m2": (ml_dtypes.float8_e5m2, 14)}[fmt]
    v = np.moveaxis(np.asarray(x, np.float32).astype(ml_dtypes.bfloat16).astype(np.float64), axis, -1)
    blocks = v.reshape(v.shape[:-1] + (-1, 32))
    amax = np.abs(blocks).max(-1, keepdims=True)
    byte = np.maximum(np.where(amax > 0, np.frexp(amax)[1] - 1 + 127, 0) - down, 1)
    scale = np.exp2(byte - 127.0)
    codes = (blocks / scale).astype(np.float32).astype(dtype).astype(np.float64)
    return np.moveaxis((codes * scale).reshape(v.shape), -1, axis)


WIDE = False


def mx_kscale(k):
    if not WIDE:
        return np.ones(k)
    levels = np.array([10, -10, 5, -5, 0])
    if k % 512:
        return np.exp2(np.random.permutation(np.resize(levels, k // 32))).repeat(32)
    a = np.empty((k // 512, 16))
    for p in range(k // 512):
        a[p, :8] = np.random.permutation(np.resize(levels, 8))
        for g in range(8):
            far = levels[np.abs(levels - a[p, g]) >= 10]
            a[p, g + 8] = far[np.random.randint(len(far))]
    return np.exp2(a.ravel()).repeat(32)


def f64(x):
    return np.asarray(x).astype(np.float64)


def striped(idx):
    return np.tile(idx.reshape(-1, 16).T, (8, 1)).astype(np.uint16)


def unstriped(offs):
    return offs[:16].T.reshape(-1).astype(np.int64)


E2M1 = np.array([0.0, 0.5, 1.0, 1.5, 2.0, 3.0, 4.0, 6.0, -0.0, -0.5, -1.0, -1.5, -2.0, -3.0, -4.0, -6.0])


def pack_weight(w, fmt):
    k, n = w.shape
    w = f64(np.asarray(w, np.float32).astype(ml_dtypes.bfloat16)).reshape(k // 32, 32, n)
    amax = np.abs(w).max(1)
    if fmt == "e4m3":
        byte = np.frexp(amax)[1] - 1 + 127 - 7
    else:
        mant, ex = np.frexp(amax / 6.0)
        byte = np.where(mant > 0.5, ex, ex - 1) + 127
    byte = np.clip(np.where(amax > 0, byte, 1), 1, 254)
    scaled = (w * np.exp2(127.0 - byte)[:, None, :]).reshape(k, n).astype(np.float32)
    by_word = np.ascontiguousarray(scaled.reshape(k // 512, 128, 4, n).transpose(0, 1, 3, 2))
    if fmt == "e4m3":
        words = by_word.astype(ml_dtypes.float8_e4m3fn).view(np.uint8)
    else:
        c = by_word.astype(ml_dtypes.float4_e2m1fn).view(np.uint8) & 0xF
        words = (c[..., 0::2] | (c[..., 1::2] << 4)).reshape(k // 512, 128, 2 * n)
    return np.ascontiguousarray(words), np.ascontiguousarray(byte.astype(np.uint8).reshape(k // 512, 16, n))


def unpack_weight(words, scales, fmt):
    g, _, n = scales.shape
    words = np.ascontiguousarray(words).reshape(g, 128, n, -1)
    if fmt == "e4m3":
        vals = words.view(ml_dtypes.float8_e4m3fn).astype(np.float64)
    else:
        nib = np.empty((g, 128, n, 4), np.uint8)
        nib[..., 0::2] = words & 0xF
        nib[..., 1::2] = words >> 4
        vals = E2M1[nib]
    vals = vals * np.repeat(np.exp2(scales.astype(np.float64) - 127.0), 8, axis=1)[..., None]
    return vals.transpose(0, 1, 3, 2).reshape(g * 512, n)


def gelu(v):
    return 0.5 * v * (1.0 + np.tanh(np.sqrt(2.0 / np.pi) * (v + 0.044715 * v**3)))


K, T, S, P, H, N = 512, 4096, 1024, 512, 1024, 768

def setup_inputs():
    n = np.random.standard_normal
    s = mx_kscale(K)[:, None]
    u = mx_kscale(H)[:, None]
    tab_words, tab_scales = pack_weight(n((K, T)) * s, "e4m3")
    w4_words, w4_scales = pack_weight(0.75 * n((K, H)) / np.sqrt(K) / s, "e2m1")
    w6_words, w6_scales = pack_weight(0.7 * n((K, N)) / np.sqrt(K) / s, "e4m3")
    perm = np.random.permutation(S)
    return {
        "tab_words": tab_words, "tab_scales": tab_scales,
        "offs": striped(np.random.permutation(T)[:S]),
        "pos1": striped(perm[:P]), "pos2": striped(perm[P:]),
        "w1": (0.75 * n((K, H)) / np.sqrt(K) / s).astype(np.float32),
        "w4_words": w4_words, "w4_scales": w4_scales,
        "bias": (0.3 * n(H)).astype(np.float32),
        "temp": np.random.uniform(0.4, 1.6, H).astype(np.float32),
        "tpl": (5.0 * n((H, P))).astype(np.float32),
        "mid": (0.5 * n(H)).astype(np.float32),
        "wgs": np.exp(0.3 * n((128, P))).astype(np.float32),
        "gain": (np.random.uniform(0.6, 1.6, H) * u[:, 0]).astype(np.float32),
        "w3": (n((H, N)) / np.sqrt(H) / u).astype(np.float32),
        "w6_words": w6_words, "w6_scales": w6_scales,
    }

def reference(tab_words, tab_scales, offs, pos1, pos2, w1, w4_words, w4_scales, bias, temp, tpl, mid, wgs, gain, w3, w6_words, w6_scales):
    v = unpack_weight(tab_words, tab_scales, "e4m3")[:, unstriped(offs)]
    w4 = unpack_weight(w4_words, w4_scales, "e2m1")
    w6 = unpack_weight(w6_words, w6_scales, "e4m3")
    plain = mxq(f64(w1), 0, "e4m3").T @ v
    typed = w4.T @ v
    h = np.maximum(plain, typed + f64(bias)[:, None])
    top = h.max(axis=1)
    look = np.exp(f64(temp)[:, None] * (h[:, unstriped(pos1)] - top[:, None]))
    a = f64(tpl) * look
    page = h - f64(mid)[:, None]
    page[:, unstriped(pos2)] = np.tile(f64(wgs), (H // 128, 1)) * a
    f = mxq(f64(gain)[:, None] * page, 0, "e4m3")
    return mxq(f64(w3), 0, "e4m3").T @ f + w6.T @ v

@@ -1,0 +1,299 @@
+from contextlib import ExitStack
+
+import concourse.mybir as mybir
+
+K, T, S, NP, H, N = 512, 4096, 1024, 512, 1024, 768
+FLOPS = 2 * S * (2 * K * H + H * N + K * N)
+
+F32 = mybir.dt.float32
+BF16 = mybir.dt.bfloat16
+I32 = mybir.dt.int32
+U32 = mybir.dt.uint32
+U16 = mybir.dt.uint16
+U8 = mybir.dt.uint8
+FP8X4 = mybir.dt.float8_e4m3fn_x4
+FP4X4 = mybir.dt.float4_e2m1fn_x4
+ALU = mybir.AluOpType
+ACT = mybir.ActivationFunctionType
+
+P = 128
+PACK = 4
+HALF = 512
+PASSES = H // (P * PACK)
+TILES = PASSES * PACK
+N_TILES = N // P
+W3_CHUNK = 256
+
+
+def tile_list_placeholder_fill_kernel(tc, tab_words, tab_scales, offs, pos1, pos2, w1, w4_words, w4_scales,
+                                                bias, temp, tpl, mid, wgs, gain, w3, w6_words, w6_scales, out):
+    nc = tc.nc
+    with ExitStack() as ctx:
+        keep = ctx.enter_context(tc.tile_pool(name="keep", bufs=1))
+        work = ctx.enter_context(tc.tile_pool(name="work", bufs=1))
+        psum = ctx.enter_context(tc.psum_pool(name="psum", bufs=1))
+
+        def held(shape, dtype, name):
+            return keep.tile(shape, dtype, name=name, align_bytes=64)
+
+        def ring(shape, dtype, name, bufs):
+            return work.tile(shape, dtype, name=name, tag=name, bufs=bufs, align_bytes=64)
+
+        def load_scale_rows(queue, plane, rows):
+            for q in range(4):
+                queue.dma_start(out=plane[32 * q : 32 * q + 4, :].bitcast(I32), in_=rows[0, 4 * q : 4 * q + 4, :].bitcast(I32))
+
+        def load_row_values(vec, name):
+            tile = held([P, TILES], F32, name)
+            nc.gpsimd.dma_start(out=tile[:].rearrange("p (b t) -> p b t", t=PACK),
+                                in_=vec.rearrange("(b p t) -> p b t", b=PASSES, t=PACK))
+            return tile
+
+        offs_sb = keep.tile([P, S // 16], U16, name="offs_sb")
+        pos1_sb = keep.tile([P, NP // 16], U16, name="pos1_sb")
+        pos2_sb = keep.tile([P, NP // 16], U16, name="pos2_sb")
+
+        def shared(shape, dtype, name, tag, bufs):
+            return work.tile(shape, dtype, name=name, tag=tag, bufs=bufs, align_bytes=64)
+
+        tab_w = shared([P, T], U32, "tab_w", "table", 1)
+        tab_s = shared([P, T], U8, "tab_s", "wide", 2)
+        w4_raw = shared([P, 2 * H], U8, "w4_raw", "narrow", 2)
+        w4_sraw = shared([P, H], U8, "w4_sraw", "narrow", 2)
+        w1_raw, w3_raw, tpl_sb = {}, {}, {}
+
+        nc.vector.memset(tab_s[:].bitcast(I32), 0)
+        nc.gpsimd.memset(w4_sraw[:].bitcast(I32), 0)
+
+        def load_w1(b):
+            w1_raw[b] = shared([P, PACK, HALF], F32, "w1_raw", "wide", 2)
+            nc.sync.dma_start(out=w1_raw[b][:], in_=w1[:, b * HALF : (b + 1) * HALF].rearrange("(p j) c -> p j c", j=PACK))
+
+        def load_tpl(i):
+            b, t = divmod(i, PACK)
+            tpl_sb[i] = shared([P, NP], F32, "tpl_sb", "narrow", 2)
+            nc.sync.dma_start(out=tpl_sb[i][:], in_=tpl[b * 512 : (b + 1) * 512, :].rearrange("(p t) m -> p t m", t=PACK)[:, t, :])
+
+        def load_w3(b, tag, bufs):
+            w3_raw[b] = shared([P, PACK, N], F32, "w3_raw", tag, bufs)
+            nc.sync.dma_start(out=w3_raw[b][:], in_=w3[b * 512 : (b + 1) * 512, :].rearrange("(p t) n -> p t n", t=PACK))
+
+        load_w1(0)
+        load_scale_rows(nc.sync, tab_s, tab_scales)
+        nc.sync.dma_start(offs_sb[:], offs)
+        nc.sync.dma_start(out=w4_raw[:].bitcast(I32), in_=w4_words[0].bitcast(I32))
+        nc.sync.dma_start(out=tab_w[:].bitcast(I32), in_=tab_words[0].rearrange("p t i -> p (t i)").bitcast(I32))
+        nc.sync.dma_start(pos1_sb[:], pos1)
+        nc.sync.dma_start(pos2_sb[:], pos2)
+        load_scale_rows(nc.scalar, w4_sraw, w4_scales)
+        bias_sb = load_row_values(bias, "bias_sb")
+        mid_sb = load_row_values(mid, "mid_sb")
+        temp_sb = load_row_values(temp, "temp_sb")
+        gain_sb = load_row_values(gain, "gain_sb")
+
+        w4_q = held([P, 2 * H], U8, "w4_q")
+        w4_s = held([P, H], U8, "w4_s")
+        nc.vector.tensor_copy(out=w4_q[:].bitcast(U16).rearrange("p (b t m) -> p b m t", b=PASSES, t=PACK),
+                              in_=w4_raw[:].bitcast(U16).rearrange("p (b m t) -> p b m t", b=PASSES, t=PACK))
+        for i in range(TILES):
+            b, t = divmod(i, PACK)
+            nc.gpsimd.tensor_copy(out=w4_s[:, P * i : P * (i + 1)],
+                                  in_=w4_sraw[:].rearrange("p (b m t) -> p b t m", b=PASSES, t=PACK)[:, b, t, :])
+
+        w1_q = [held([P, HALF], U32, "w1_q%d" % b) for b in range(PASSES)]
+        w1_s = [shared([P, HALF], U8, "w1_s%d" % b, "plane%d" % b, 1) for b in range(PASSES)]
+
+        w1_g = {}
+
+        def quantise_w1(b, u):
+            if u == 0:
+                w1_g[b] = shared([P, PACK, P, PACK], BF16, "w1_g", "grouped", 1)
+            nc.scalar.copy(out=w1_g[b][:, :, 64 * u : 64 * (u + 1), :].rearrange("p t m j -> p m j t"),
+                           in_=w1_raw[b][:, :, 256 * u : 256 * (u + 1)].rearrange("p j (m t) -> p m j t", t=PACK))
+            if u == 1:
+                nc.vector.quantize_mx(out=w1_q[b][:].bitcast(FP8X4), scales=w1_s[b][:],
+                                      in_=w1_g[b][:].rearrange("p t m j -> p (t m j)"))
+
+        quantise_w1(0, 0)
+        quantise_w1(0, 1)
+
+        v_q = [held([P, HALF], U32, "v_q%d" % c) for c in range(2)]
+        v_s = [held([P, HALF], U8, "v_s%d" % c) for c in range(2)]
+        for c in range(2):
+            nc.vector.tensor_copy(v_s[c][:], tab_s[:].indirect(offs_sb[:, 32 * c : 32 * (c + 1)]))
+        for c in range(2):
+            nc.vector.tensor_copy(v_q[c][:], tab_w[:].indirect(offs_sb[:, 32 * c : 32 * (c + 1)]))
+
+        load_tpl(0)
+        wgs_sb = shared([P, PACK, NP], F32, "wgs_sb", "wide", 2)
+        for q in range(4):
+            nc.sync.dma_start(out=wgs_sb[32 * q : 32 * q + 32, :, :], in_=wgs.rearrange("(q t) m -> q t m", t=PACK))
+        load_tpl(1)
+        load_w1(1)
+        load_w3(0, "table", 1)
+        w6 = {}
+
+        def load_w6_words():
+            w6["q"] = shared([P, N], U32, "w6_q", "grouped", 1)
+            nc.sync.dma_start(out=w6["q"][:].bitcast(I32), in_=w6_words[0].rearrange("p c i -> p (c i)").bitcast(I32))
+
+        def load_w6_scales():
+            w6["s"] = shared([P, N], U8, "w6_s", "plane0", 1)
+            nc.gpsimd.memset(w6["s"][:].bitcast(I32), 0)
+            load_scale_rows(nc.sync, w6["s"], w6_scales)
+
+        neg_temp = held([P, TILES], F32, "neg_temp")
+        neg_temp_mid = held([P, TILES], F32, "neg_temp_mid")
+        nc.gpsimd.tensor_scalar(neg_temp[:], temp_sb[:], -1.0, 0.0, ALU.mult, ALU.add)
+        nc.gpsimd.tensor_tensor(neg_temp_mid[:], neg_temp[:], mid_sb[:], ALU.mult)
+        page_top = held([P, TILES], F32, "page_top")
+        look_bias = held([P, TILES], F32, "look_bias")
+
+        w3_q = [held([P, N], U32, "w3_q%d" % b) for b in range(PASSES)]
+        w3_s = [held([P, N], U8, "w3_s%d" % b) for b in range(PASSES)]
+
+        def quantise_w3(b, u):
+            cols = slice(u * W3_CHUNK, (u + 1) * W3_CHUNK)
+            w3_g = ring([P, W3_CHUNK, PACK], BF16, "w3_g", 3)
+            nc.scalar.copy(out=w3_g[:].rearrange("p (c i) t -> p c t i", i=4),
+                           in_=w3_raw[b][:, :, cols].rearrange("p t (c i) -> p c t i", i=4))
+            nc.vector.quantize_mx(out=w3_q[b][:, cols].bitcast(FP8X4), scales=w3_s[b][:, cols],
+                                  in_=w3_g[:].rearrange("p c t -> p (c t)"))
+
+        scaled = [[held([P, PACK, HALF], BF16, "scaled%d_%d" % (b, c)) for c in range(2)] for b in range(PASSES)]
+        f_q = [[held([P, HALF], U32, "f_q%d_%d" % (b, c)) for c in range(2)] for b in range(PASSES)]
+        f_s = [[held([P, HALF], U8, "f_s%d_%d" % (b, c)) for c in range(2)] for b in range(PASSES)]
+        pages, looks, weights = {}, {}, {}
+
+        readings = {}
+
+        def read_tile(i):
+            b, t = divmod(i, PACK)
+            col = slice(i, i + 1)
+            h = ring([P, S], F32, "h", 3)
+            for c in range(2):
+                typed = psum.tile([P, HALF], F32, name="typed", tag="bank%d" % c)
+                plain = psum.tile([P, HALF], F32, name="plain", tag="bank%d" % (2 + c))
+                nc.tensor.matmul_mx(out=typed[:], lhsT=w4_q[:, 2 * P * i : 2 * P * (i + 1)].bitcast(FP4X4),
+                                    lhsT_scale=w4_s[:, P * i : P * (i + 1)], rhs=v_q[c][:].bitcast(FP8X4),
+                                    rhs_scale=v_s[c][:], start=True, stop=True)
+                nc.tensor.matmul_mx(out=plain[:], lhsT=w1_q[b][:, P * t : P * (t + 1)].bitcast(FP8X4),
+                                    lhsT_scale=w1_s[b][:, P * t : P * (t + 1)], rhs=v_q[c][:].bitcast(FP8X4),
+                                    rhs_scale=v_s[c][:], start=True, stop=True)
+                biased = shared([P, HALF], F32, "biased", "turn%d_%d" % (c, i % 2), 1)
+                nc.scalar.activation(out=biased[:], in_=typed[:], func=ACT.Identity, bias=bias_sb[:, col])
+                nc.vector.tensor_tensor(h[:, c * HALF : (c + 1) * HALF], plain[:], biased[:], ALU.max)
+            page = ring([P, S], F32, "page", 3)
+            nc.vector.tensor_scalar(page[:], h[:], mid_sb[:, col], None, ALU.subtract, ALU.max, accum_out=page_top[:, col])
+            pages[i], readings[i] = page, h
+
+        def look_tile(i):
+            col = slice(i, i + 1)
+            nc.scalar.activation(out=look_bias[:, col], in_=page_top[:, col], func=ACT.Identity,
+                                 bias=neg_temp_mid[:, col], scale=neg_temp[:, col])
+            looks[i] = ring([P, NP], F32, "look", 3)
+            nc.scalar.activation(out=looks[i][:], in_=readings[i][:].indirect(pos1_sb[:]), func=ACT.Exp,
+                                 bias=look_bias[:, col], scale=temp_sb[:, col])
+
+        def weigh_tile(i):
+            weights[i] = shared([P, NP], F32, "weight", "turn0_%d" % ((i + 1) % 2), 1)
+            nc.gpsimd.tensor_tensor(weights[i][:], tpl_sb[i][:], wgs_sb[:, i % PACK, :], ALU.mult)
+
+        def fill_tile(i):
+            nc.vector.tensor_tensor(pages[i][:].indirect(pos2_sb[:]), looks[i][:], weights[i][:], ALU.mult)
+
+        def scale_tile(i, c, on_vector):
+            b, t = divmod(i, PACK)
+            src = pages[i][:, c * HALF : (c + 1) * HALF]
+            if on_vector:
+                nc.vector.tensor_scalar(scaled[b][c][:, t, :], src, gain_sb[:, i : i + 1], None, ALU.mult)
+            else:
+                nc.scalar.activation(out=scaled[b][c][:, t, :], in_=src, func=ACT.Copy, scale=gain_sb[:, i : i + 1])
+
+        f_g = {}
+
+        def quantise_f(b, c, u, on_vector):
+            if u == 0:
+                f_g[b, c] = ring([P, HALF, PACK], BF16, "f_g", 2)
+            cols = slice(256 * u, 256 * (u + 1))
+            dst = f_g[b, c][:, cols, :].rearrange("p (c i) t -> p c t i", i=4)
+            src = scaled[b][c][:, :, cols].rearrange("p t (c i) -> p c t i", i=4)
+            if on_vector:
+                nc.vector.tensor_copy(out=dst, in_=src)
+            else:
+                nc.scalar.copy(out=dst, in_=src)
+            if u == 1:
+                nc.vector.quantize_mx(out=f_q[b][c][:].bitcast(FP8X4), scales=f_s[b][c][:],
+                                      in_=f_g[b, c][:].rearrange("p c t -> p (c t)"))
+
+        sums = {}
+
+        def open_sum(c, n, bank):
+            cols = slice(n * P, (n + 1) * P)
+            acc = psum.tile([P, HALF], F32, name="acc", tag="bank%d" % bank)
+            nc.tensor.matmul_mx(out=acc[:], lhsT=w6["q"][:, cols].bitcast(FP8X4), lhsT_scale=w6["s"][:, cols],
+                                rhs=v_q[c][:].bitcast(FP8X4), rhs_scale=v_s[c][:], start=True, stop=False)
+            nc.tensor.matmul_mx(out=acc[:], lhsT=w3_q[0][:, cols].bitcast(FP8X4), lhsT_scale=w3_s[0][:, cols],
+                                rhs=f_q[0][c][:].bitcast(FP8X4), rhs_scale=f_s[0][c][:], start=False, stop=False)
+            sums[c, n] = acc
+
+        def close_sum(c, n, on_vector):
+            cols = slice(n * P, (n + 1) * P)
+            acc = sums[c, n]
+            nc.tensor.matmul_mx(out=acc[:], lhsT=w3_q[1][:, cols].bitcast(FP8X4), lhsT_scale=w3_s[1][:, cols],
+                                rhs=f_q[1][c][:].bitcast(FP8X4), rhs_scale=f_s[1][c][:], start=False, stop=True)
+            result = ring([P, HALF], F32, "result", 8)
+            if on_vector:
+                nc.vector.tensor_copy(out=result[:], in_=acc[:])
+            else:
+                nc.scalar.copy(out=result[:], in_=acc[:])
+            nc.sync.dma_start(out=out[cols, c * HALF : (c + 1) * HALF], in_=result[:])
+
+        def side_work(i):
+            if i == 2:
+                quantise_w1(1, 0)
+                quantise_w1(1, 1)
+                load_w3(1, "wide", 2)
+                load_w6_words()
+            if i == 3:
+                quantise_w3(0, 0)
+                quantise_w3(0, 1)
+            if i == 4:
+                load_w6_scales()
+                quantise_w3(0, 2)
+                quantise_w3(1, 0)
+            if i in (5, 6):
+                quantise_f(0, i - 5, 0, False)
+                quantise_f(0, i - 5, 1, False)
+            if i == 7:
+                quantise_w3(1, 1)
+                quantise_w3(1, 2)
+
+        for i in range(TILES + 1):
+            if i < TILES:
+                read_tile(i)
+            if i >= 2:
+                for c in range(2):
+                    scale_tile(i - 2, c, False)
+            if i < TILES:
+                look_tile(i)
+            side_work(i)
+            if i >= 1:
+                weigh_tile(i - 1)
+                if i + 1 < TILES:
+                    load_tpl(i + 1)
+                fill_tile(i - 1)
+        order = [(c, n) for c in range(2) for n in range(N_TILES)]
+        banks = [4, 5, 6, 7, 0, 1, 2, 3]
+        for k in range(8):
+            open_sum(*order[k], banks[k])
+        scale_tile(TILES - 1, 0, True)
+        scale_tile(TILES - 1, 1, False)
+        for u in range(2):
+            quantise_f(1, 0, u, True)
+        for u in range(2):
+            quantise_f(1, 1, u, False)
+        for k in range(len(order)):
+            close_sum(*order[k], k % 2 == 0)
+            if k + 8 < len(order):
+                open_sum(*order[k + 8], banks[k])

@@ -23,6 +23,7 @@ PASSES = H // (P * PACK)
 TILES = PASSES * PACK
 N_TILES = N // P
 W3_CHUNK = 256
+SIDE = {0:(0,1),1:(2,3),2:(4,5),3:(6,7),4:(8,9)}
 
 
 def tile_list_placeholder_fill_kernel(tc, tab_words, tab_scales, offs, pos1, pos2, w1, w4_words, w4_scales,
@@ -39,261 +40,288 @@ def tile_list_placeholder_fill_kernel(tc, tab_words, tab_scales, offs, pos1, pos
         def ring(shape, dtype, name, bufs):
             return work.tile(shape, dtype, name=name, tag=name, bufs=bufs, align_bytes=64)
 
-        def load_scale_rows(queue, plane, rows):
-            for q in range(4):
-                queue.dma_start(out=plane[32 * q : 32 * q + 4, :].bitcast(I32), in_=rows[0, 4 * q : 4 * q + 4, :].bitcast(I32))
+        def shared(shape, dtype, name, tag, bufs):
+            return work.tile(shape, dtype, name=name, tag=tag, bufs=bufs, align_bytes=64)
 
-        def load_row_values(vec, name):
+        def load_scale_rows(queue, plane, rows):
+            for r in range(4):
+                queue.dma_start(out=plane[r:P:32, :].bitcast(I32), in_=rows[0, r:16:4, :].bitcast(I32))
+
+        def load_row_values(queue, vec, name):
             tile = held([P, TILES], F32, name)
-            nc.gpsimd.dma_start(out=tile[:].rearrange("p (b t) -> p b t", t=PACK),
-                                in_=vec.rearrange("(b p t) -> p b t", b=PASSES, t=PACK))
+            queue.dma_start(out=tile[:].rearrange("p (b t) -> p b t", t=PACK),
+                            in_=vec.rearrange("(b p t) -> p b t", b=PASSES, t=PACK))
             return tile
 
         offs_sb = keep.tile([P, S // 16], U16, name="offs_sb")
         pos1_sb = keep.tile([P, NP // 16], U16, name="pos1_sb")
         pos2_sb = keep.tile([P, NP // 16], U16, name="pos2_sb")
-
-        def shared(shape, dtype, name, tag, bufs):
-            return work.tile(shape, dtype, name=name, tag=tag, bufs=bufs, align_bytes=64)
-
-        tab_w = shared([P, T], U32, "tab_w", "table", 1)
-        tab_s = shared([P, T], U8, "tab_s", "wide", 2)
-        w4_raw = shared([P, 2 * H], U8, "w4_raw", "narrow", 2)
-        w4_sraw = shared([P, H], U8, "w4_sraw", "narrow", 2)
-        w1_raw, w3_raw, tpl_sb = {}, {}, {}
+        tab_w = held([P, T], U32, "tab_w")
+        tab_s = held([P, T], U8, "tab_s")
+        w4_raw = held([P, 2 * H], U8, "w4_raw")
+        w4_sraw = held([P, H], U8, "w4_sraw")
+        w6_q = held([P, N], U32, "w6_q")
+        w6_s = held([P, N], U8, "w6_s")
+        w1_raw = [held([P, PACK, HALF], F32, "w1_raw%d" % b) for b in range(PASSES)]
+        w3_raw = [held([P, PACK, N], F32, "w3_raw%d" % b) for b in range(PASSES)]
+        tpl_sb = [shared([P, NP], F32, "tpl%d" % i, "small%d" % i, 1) for i in range(TILES)]
+        wgs_sb = held([P, PACK, NP], F32, "wgs_sb")
 
         nc.vector.memset(tab_s[:].bitcast(I32), 0)
         nc.gpsimd.memset(w4_sraw[:].bitcast(I32), 0)
+        nc.vector.memset(w6_s[:].bitcast(I32), 0)
 
         def load_w1(b):
-            w1_raw[b] = shared([P, PACK, HALF], F32, "w1_raw", "wide", 2)
             nc.sync.dma_start(out=w1_raw[b][:], in_=w1[:, b * HALF : (b + 1) * HALF].rearrange("(p j) c -> p j c", j=PACK))
 
         def load_tpl(i):
             b, t = divmod(i, PACK)
-            tpl_sb[i] = shared([P, NP], F32, "tpl_sb", "narrow", 2)
             nc.sync.dma_start(out=tpl_sb[i][:], in_=tpl[b * 512 : (b + 1) * 512, :].rearrange("(p t) m -> p t m", t=PACK)[:, t, :])
 
-        def load_w3(b, tag, bufs):
-            w3_raw[b] = shared([P, PACK, N], F32, "w3_raw", tag, bufs)
+        def load_w3(b):
             nc.sync.dma_start(out=w3_raw[b][:], in_=w3[b * 512 : (b + 1) * 512, :].rearrange("(p t) n -> p t n", t=PACK))
 
-        load_w1(0)
-        load_scale_rows(nc.sync, tab_s, tab_scales)
         nc.sync.dma_start(offs_sb[:], offs)
-        nc.sync.dma_start(out=w4_raw[:].bitcast(I32), in_=w4_words[0].bitcast(I32))
         nc.sync.dma_start(out=tab_w[:].bitcast(I32), in_=tab_words[0].rearrange("p t i -> p (t i)").bitcast(I32))
+        load_scale_rows(nc.sync, tab_s, tab_scales)
+        nc.sync.dma_start(out=w4_raw[:].bitcast(I32), in_=w4_words[0].bitcast(I32))
+        load_w1(0)
+        load_scale_rows(nc.gpsimd, w4_sraw, w4_scales)
+        bias_sb = load_row_values(nc.sync, bias, "bias_sb")
+        temp_sb = load_row_values(nc.sync, temp, "temp_sb")
+        mid_sb = load_row_values(nc.sync, mid, "mid_sb")
+        load_w1(1)
         nc.sync.dma_start(pos1_sb[:], pos1)
+        load_tpl(0)
+        for q in (0, 2, 1, 3):
+            nc.sync.dma_start(out=wgs_sb[32 * q : 32 * q + 32, :, :], in_=wgs.rearrange("(q t) m -> q t m", t=PACK))
         nc.sync.dma_start(pos2_sb[:], pos2)
-        load_scale_rows(nc.scalar, w4_sraw, w4_scales)
-        bias_sb = load_row_values(bias, "bias_sb")
-        mid_sb = load_row_values(mid, "mid_sb")
-        temp_sb = load_row_values(temp, "temp_sb")
-        gain_sb = load_row_values(gain, "gain_sb")
-
-        w4_q = held([P, 2 * H], U8, "w4_q")
-        w4_s = held([P, H], U8, "w4_s")
-        nc.vector.tensor_copy(out=w4_q[:].bitcast(U16).rearrange("p (b t m) -> p b m t", b=PASSES, t=PACK),
-                              in_=w4_raw[:].bitcast(U16).rearrange("p (b m t) -> p b m t", b=PASSES, t=PACK))
-        for i in range(TILES):
-            b, t = divmod(i, PACK)
-            nc.gpsimd.tensor_copy(out=w4_s[:, P * i : P * (i + 1)],
-                                  in_=w4_sraw[:].rearrange("p (b m t) -> p b t m", b=PASSES, t=PACK)[:, b, t, :])
-
-        w1_q = [held([P, HALF], U32, "w1_q%d" % b) for b in range(PASSES)]
-        w1_s = [shared([P, HALF], U8, "w1_s%d" % b, "plane%d" % b, 1) for b in range(PASSES)]
-
-        w1_g = {}
-
-        def quantise_w1(b, u):
-            if u == 0:
-                w1_g[b] = shared([P, PACK, P, PACK], BF16, "w1_g", "grouped", 1)
-            nc.scalar.copy(out=w1_g[b][:, :, 64 * u : 64 * (u + 1), :].rearrange("p t m j -> p m j t"),
-                           in_=w1_raw[b][:, :, 256 * u : 256 * (u + 1)].rearrange("p j (m t) -> p m j t", t=PACK))
-            if u == 1:
-                nc.vector.quantize_mx(out=w1_q[b][:].bitcast(FP8X4), scales=w1_s[b][:],
-                                      in_=w1_g[b][:].rearrange("p t m j -> p (t m j)"))
-
-        quantise_w1(0, 0)
-        quantise_w1(0, 1)
+        gain_sb = load_row_values(nc.sync, gain, "gain_sb")
+        load_tpl(1)
+        load_tpl(2)
+        load_tpl(3)
+        load_w3(0)
+        for i in range(PACK, TILES):
+            load_tpl(i)
+        load_w3(1)
+        nc.sync.dma_start(out=w6_q[:].bitcast(I32), in_=w6_words[0].rearrange("p c i -> p (c i)").bitcast(I32))
+        load_scale_rows(nc.sync, w6_s, w6_scales)
 
         v_q = [held([P, HALF], U32, "v_q%d" % c) for c in range(2)]
         v_s = [held([P, HALF], U8, "v_s%d" % c) for c in range(2)]
         for c in range(2):
-            nc.vector.tensor_copy(v_s[c][:], tab_s[:].indirect(offs_sb[:, 32 * c : 32 * (c + 1)]))
-        for c in range(2):
             nc.vector.tensor_copy(v_q[c][:], tab_w[:].indirect(offs_sb[:, 32 * c : 32 * (c + 1)]))
+        for c in range(2):
+            nc.vector.tensor_copy(v_s[c][:], tab_s[:].indirect(offs_sb[:, 32 * c : 32 * (c + 1)]))
 
-        load_tpl(0)
-        wgs_sb = shared([P, PACK, NP], F32, "wgs_sb", "wide", 2)
-        for q in range(4):
-            nc.sync.dma_start(out=wgs_sb[32 * q : 32 * q + 32, :, :], in_=wgs.rearrange("(q t) m -> q t m", t=PACK))
-        load_tpl(1)
-        load_w1(1)
-        load_w3(0, "table", 1)
-        w6 = {}
+        w4_q = held([P, 2 * H], U8, "w4_q")
+        w4_s = held([P, H], U8, "w4_s")
+        nc.scalar.copy(out=w4_q[:].bitcast(U16).rearrange("p (b t m) -> p b m t", b=PASSES, t=PACK),
+                       in_=w4_raw[:].bitcast(U16).rearrange("p (b m t) -> p b m t", b=PASSES, t=PACK))
+        for b in range(PASSES):
+            cols = slice(b * HALF, (b + 1) * HALF)
+            nc.gpsimd.tensor_copy(out=w4_s[:, cols].rearrange("p (t m) -> p t m", t=PACK),
+                                  in_=w4_sraw[:, cols].rearrange("p (m t) -> p t m", t=PACK))
 
-        def load_w6_words():
-            w6["q"] = shared([P, N], U32, "w6_q", "grouped", 1)
-            nc.sync.dma_start(out=w6["q"][:].bitcast(I32), in_=w6_words[0].rearrange("p c i -> p (c i)").bitcast(I32))
+        w1_q = [held([P, HALF], U32, "w1_q%d" % b) for b in range(PASSES)]
+        w1_s = [held([P, HALF], U8, "w1_s%d" % b) for b in range(PASSES)]
+        w1_g = {}
 
-        def load_w6_scales():
-            w6["s"] = shared([P, N], U8, "w6_s", "plane0", 1)
-            nc.gpsimd.memset(w6["s"][:].bitcast(I32), 0)
-            load_scale_rows(nc.sync, w6["s"], w6_scales)
+        w1_one = held([P, P, PACK], BF16, "w1_one")
+        w1_first = w1_raw[0][:].rearrange("p j (m t) -> p t m j", t=PACK)[:, 0, :, :]
+        nc.scalar.copy(out=w1_one[:, : P // 2, :], in_=w1_first[:, : P // 2, :])
+        nc.vector.tensor_copy(out=w1_one[:, P // 2 :, :], in_=w1_first[:, P // 2 :, :])
+        nc.vector.quantize_mx(out=w1_q[0][:, :P].bitcast(FP8X4), scales=w1_s[0][:, :P], in_=w1_one[:].rearrange("p m j -> p (m j)"))
+
+        def quantise_w1(b, u):
+            first = 1 - b
+            if u == 0:
+                w1_g[b] = ring([P, PACK, P, PACK], BF16, "w1_g", 1)
+            nc.scalar.copy(out=w1_g[b][:, first:, 64 * u : 64 * (u + 1), :].rearrange("p t m j -> p m j t"),
+                           in_=w1_raw[b][:, :, 256 * u : 256 * (u + 1)].rearrange("p j (m t) -> p m j t", t=PACK)[:, :, :, first:])
+            if u == 1:
+                nc.vector.quantize_mx(out=w1_q[b][:, first * P :].bitcast(FP8X4), scales=w1_s[b][:, first * P :],
+                                      in_=w1_g[b][:, first:, :, :].rearrange("p t m j -> p (t m j)"))
 
         neg_temp = held([P, TILES], F32, "neg_temp")
-        neg_temp_mid = held([P, TILES], F32, "neg_temp_mid")
-        nc.gpsimd.tensor_scalar(neg_temp[:], temp_sb[:], -1.0, 0.0, ALU.mult, ALU.add)
-        nc.gpsimd.tensor_tensor(neg_temp_mid[:], neg_temp[:], mid_sb[:], ALU.mult)
         page_top = held([P, TILES], F32, "page_top")
         look_bias = held([P, TILES], F32, "look_bias")
 
-        w3_q = [held([P, N], U32, "w3_q%d" % b) for b in range(PASSES)]
         w3_s = [held([P, N], U8, "w3_s%d" % b) for b in range(PASSES)]
+        w3_g, w3_q, f_q, f_g = {}, {}, {}, {}
 
-        def quantise_w3(b, u):
+        def group_w3(b, u):
+            if u == 0:
+                w3_g[b] = held([P, N, PACK], BF16, "w3_g%d" % b)
             cols = slice(u * W3_CHUNK, (u + 1) * W3_CHUNK)
-            w3_g = ring([P, W3_CHUNK, PACK], BF16, "w3_g", 3)
-            nc.scalar.copy(out=w3_g[:].rearrange("p (c i) t -> p c t i", i=4),
+            nc.scalar.copy(out=w3_g[b][:, cols, :].rearrange("p (c i) t -> p c t i", i=4),
                            in_=w3_raw[b][:, :, cols].rearrange("p t (c i) -> p c t i", i=4))
-            nc.vector.quantize_mx(out=w3_q[b][:, cols].bitcast(FP8X4), scales=w3_s[b][:, cols],
-                                  in_=w3_g[:].rearrange("p c t -> p (c t)"))
+
+        def quantise_w3(b):
+            for u in range(2):
+                cols = slice(u * N // 2, (u + 1) * N // 2)
+                nc.vector.quantize_mx(out=w3_q[b][:, cols].bitcast(FP8X4), scales=w3_s[b][:, cols],
+                                      in_=w3_g[b][:, cols, :].rearrange("p c t -> p (c t)"))
 
         scaled = [[held([P, PACK, HALF], BF16, "scaled%d_%d" % (b, c)) for c in range(2)] for b in range(PASSES)]
-        f_q = [[held([P, HALF], U32, "f_q%d_%d" % (b, c)) for c in range(2)] for b in range(PASSES)]
         f_s = [[held([P, HALF], U8, "f_s%d_%d" % (b, c)) for c in range(2)] for b in range(PASSES)]
         pages, looks, weights = {}, {}, {}
 
         readings = {}
 
-        def read_tile(i):
-            b, t = divmod(i, PACK)
-            col = slice(i, i + 1)
-            h = ring([P, S], F32, "h", 3)
+        biased = {}
+
+        def read_typed(i):
             for c in range(2):
                 typed = psum.tile([P, HALF], F32, name="typed", tag="bank%d" % c)
-                plain = psum.tile([P, HALF], F32, name="plain", tag="bank%d" % (2 + c))
                 nc.tensor.matmul_mx(out=typed[:], lhsT=w4_q[:, 2 * P * i : 2 * P * (i + 1)].bitcast(FP4X4),
                                     lhsT_scale=w4_s[:, P * i : P * (i + 1)], rhs=v_q[c][:].bitcast(FP8X4),
                                     rhs_scale=v_s[c][:], start=True, stop=True)
+                biased[i, c] = ring([P, HALF], F32, "biased", 4)
+                nc.scalar.activation(out=biased[i, c][:], in_=typed[:], func=ACT.Identity, bias=bias_sb[:, i : i + 1])
+
+        def read_tile(i):
+            b, t = divmod(i, PACK)
+            h = ring([P, S], F32, "h", 3)
+            for c in range(2):
+                plain = psum.tile([P, HALF], F32, name="plain", tag="bank%d" % (2 + c))
                 nc.tensor.matmul_mx(out=plain[:], lhsT=w1_q[b][:, P * t : P * (t + 1)].bitcast(FP8X4),
                                     lhsT_scale=w1_s[b][:, P * t : P * (t + 1)], rhs=v_q[c][:].bitcast(FP8X4),
                                     rhs_scale=v_s[c][:], start=True, stop=True)
-                biased = shared([P, HALF], F32, "biased", "turn%d_%d" % (c, i % 2), 1)
-                nc.scalar.activation(out=biased[:], in_=typed[:], func=ACT.Identity, bias=bias_sb[:, col])
-                nc.vector.tensor_tensor(h[:, c * HALF : (c + 1) * HALF], plain[:], biased[:], ALU.max)
-            page = ring([P, S], F32, "page", 3)
-            nc.vector.tensor_scalar(page[:], h[:], mid_sb[:, col], None, ALU.subtract, ALU.max, accum_out=page_top[:, col])
-            pages[i], readings[i] = page, h
+                nc.vector.tensor_tensor(h[:, c * HALF : (c + 1) * HALF], plain[:], biased[i, c][:], ALU.max)
+            readings[i] = h
+
+        def centre_tile(i):
+            col = slice(i, i + 1)
+            pages[i] = ring([P, S], F32, "page", 4)
+            nc.vector.tensor_scalar(pages[i][:], readings[i][:], mid_sb[:, col], None, ALU.subtract, ALU.max,
+                                    accum_out=page_top[:, col])
+            nc.vector.tensor_scalar(look_bias[:, col], page_top[:, col], mid_sb[:, col], neg_temp[:, col], ALU.add, ALU.mult)
 
         def look_tile(i):
             col = slice(i, i + 1)
-            nc.scalar.activation(out=look_bias[:, col], in_=page_top[:, col], func=ACT.Identity,
-                                 bias=neg_temp_mid[:, col], scale=neg_temp[:, col])
             looks[i] = ring([P, NP], F32, "look", 3)
             nc.scalar.activation(out=looks[i][:], in_=readings[i][:].indirect(pos1_sb[:]), func=ACT.Exp,
                                  bias=look_bias[:, col], scale=temp_sb[:, col])
 
         def weigh_tile(i):
-            weights[i] = shared([P, NP], F32, "weight", "turn0_%d" % ((i + 1) % 2), 1)
+            weights[i] = shared([P, NP], F32, "weight", "late", 1) if i == TILES - 3 else ring([P, NP], F32, "weight", 2)
             nc.gpsimd.tensor_tensor(weights[i][:], tpl_sb[i][:], wgs_sb[:, i % PACK, :], ALU.mult)
 
         def fill_tile(i):
             nc.vector.tensor_tensor(pages[i][:].indirect(pos2_sb[:]), looks[i][:], weights[i][:], ALU.mult)
 
-        def scale_tile(i, c, on_vector):
+        def scale_tile(i, c, cols, on_vector):
             b, t = divmod(i, PACK)
-            src = pages[i][:, c * HALF : (c + 1) * HALF]
+            src = pages[i][:, c * HALF : (c + 1) * HALF][:, cols]
             if on_vector:
-                nc.vector.tensor_scalar(scaled[b][c][:, t, :], src, gain_sb[:, i : i + 1], None, ALU.mult)
+                nc.vector.tensor_scalar(scaled[b][c][:, t, cols], src, gain_sb[:, i : i + 1], None, ALU.mult)
             else:
-                nc.scalar.activation(out=scaled[b][c][:, t, :], in_=src, func=ACT.Copy, scale=gain_sb[:, i : i + 1])
+                nc.scalar.activation(out=scaled[b][c][:, t, cols], in_=src, func=ACT.Copy, scale=gain_sb[:, i : i + 1])
 
-        f_g = {}
+        quarters = [slice(0, 256), slice(256, 512)]
+        whole = slice(0, HALF)
 
-        def quantise_f(b, c, u, on_vector):
+        def group_f(b, c, u, on_vector):
             if u == 0:
-                f_g[b, c] = ring([P, HALF, PACK], BF16, "f_g", 2)
-            cols = slice(256 * u, 256 * (u + 1))
-            dst = f_g[b, c][:, cols, :].rearrange("p (c i) t -> p c t i", i=4)
-            src = scaled[b][c][:, :, cols].rearrange("p t (c i) -> p c t i", i=4)
+                f_g[b, c] = ring([P, HALF, PACK], BF16, "f_g", 3)
+            dst = f_g[b, c][:, quarters[u], :].rearrange("p (c i) t -> p c t i", i=4)
+            src = scaled[b][c][:, :, quarters[u]].rearrange("p t (c i) -> p c t i", i=4)
             if on_vector:
                 nc.vector.tensor_copy(out=dst, in_=src)
             else:
                 nc.scalar.copy(out=dst, in_=src)
-            if u == 1:
-                nc.vector.quantize_mx(out=f_q[b][c][:].bitcast(FP8X4), scales=f_s[b][c][:],
-                                      in_=f_g[b, c][:].rearrange("p c t -> p (c t)"))
 
+        def quantise_f(b, c, cols):
+            nc.vector.quantize_mx(out=f_q[b, c][:, cols].bitcast(FP8X4), scales=f_s[b][c][:, cols],
+                                  in_=f_g[b, c][:, cols, :].rearrange("p c t -> p (c t)"))
+
+        parts = [(0, quarters[u], (n, n + 1)) for u in range(2) for n in range(0, N_TILES, 2)]
+        parts = parts + [(1, whole, (n,)) for n in range(N_TILES)]
+        banks = [4, 5, 6, 7, 0, 1, 2, 3]
         sums = {}
 
-        def open_sum(c, n, bank):
-            cols = slice(n * P, (n + 1) * P)
-            acc = psum.tile([P, HALF], F32, name="acc", tag="bank%d" % bank)
-            nc.tensor.matmul_mx(out=acc[:], lhsT=w6["q"][:, cols].bitcast(FP8X4), lhsT_scale=w6["s"][:, cols],
-                                rhs=v_q[c][:].bitcast(FP8X4), rhs_scale=v_s[c][:], start=True, stop=False)
-            nc.tensor.matmul_mx(out=acc[:], lhsT=w3_q[0][:, cols].bitcast(FP8X4), lhsT_scale=w3_s[0][:, cols],
-                                rhs=f_q[0][c][:].bitcast(FP8X4), rhs_scale=f_s[0][c][:], start=False, stop=False)
-            sums[c, n] = acc
+        def add_pass(k, w_q, w_s, x_q, x_s, start, stop):
+            c, cols, rows = parts[k]
+            width = cols.stop - cols.start
+            for a, n in enumerate(rows):
+                w_cols = slice(n * P, (n + 1) * P)
+                nc.tensor.matmul_mx(out=sums[k][:, a * width : (a + 1) * width], lhsT=w_q[:, w_cols].bitcast(FP8X4),
+                                    lhsT_scale=w_s[:, w_cols], rhs=x_q[:, cols].bitcast(FP8X4), rhs_scale=x_s[:, cols],
+                                    start=start and a == 0, stop=stop and a == len(rows) - 1)
 
-        def close_sum(c, n, on_vector):
-            cols = slice(n * P, (n + 1) * P)
-            acc = sums[c, n]
-            nc.tensor.matmul_mx(out=acc[:], lhsT=w3_q[1][:, cols].bitcast(FP8X4), lhsT_scale=w3_s[1][:, cols],
-                                rhs=f_q[1][c][:].bitcast(FP8X4), rhs_scale=f_s[1][c][:], start=False, stop=True)
-            result = ring([P, HALF], F32, "result", 8)
+        def open_sum(k):
+            c = parts[k][0]
+            sums[k] = psum.tile([P, HALF], F32, name="acc", tag="bank%d" % banks[k % 8])
+            add_pass(k, w6_q, w6_s, v_q[c], v_s[c], True, False)
+            add_pass(k, w3_q[0], w3_s[0], f_q[0, c], f_s[0][c], False, False)
+
+        def close_sum(k, on_vector):
+            c, cols, rows = parts[k]
+            add_pass(k, w3_q[1], w3_s[1], f_q[1, c], f_s[1][c], False, True)
+            result = shared([P, HALF], F32, "result", "small%d" % k, 1)
             if on_vector:
-                nc.vector.tensor_copy(out=result[:], in_=acc[:])
+                nc.vector.tensor_copy(out=result[:], in_=sums[k][:])
             else:
-                nc.scalar.copy(out=result[:], in_=acc[:])
-            nc.sync.dma_start(out=out[cols, c * HALF : (c + 1) * HALF], in_=result[:])
+                nc.scalar.copy(out=result[:], in_=sums[k][:])
+            dst = out[rows[0] * P : (rows[-1] + 1) * P, c * HALF + cols.start : c * HALF + cols.stop]
+            nc.sync.dma_start(out=dst.rearrange("(a p) j -> p a j", p=P), in_=result[:].rearrange("p (a j) -> p a j", a=len(rows)))
 
-        def side_work(i):
-            if i == 2:
+        def side_work(k):
+            if k == -1:
                 quantise_w1(1, 0)
                 quantise_w1(1, 1)
-                load_w3(1, "wide", 2)
-                load_w6_words()
-            if i == 3:
-                quantise_w3(0, 0)
-                quantise_w3(0, 1)
-            if i == 4:
-                load_w6_scales()
-                quantise_w3(0, 2)
-                quantise_w3(1, 0)
-            if i in (5, 6):
-                quantise_f(0, i - 5, 0, False)
-                quantise_f(0, i - 5, 1, False)
-            if i == 7:
-                quantise_w3(1, 1)
-                quantise_w3(1, 2)
-
-        for i in range(TILES + 1):
-            if i < TILES:
-                read_tile(i)
-            if i >= 2:
+            for job in SIDE.get(k, ()):
+                if job < 6:
+                    group_w3(job // 3, job % 3)
+                else:
+                    group_f(0, (job - 6) // 2, job % 2, False)
+            if k == TILES - 3:
+                late = shared([P, 2 * N + S], U32, "late", "late", 1)
+                for b in range(PASSES):
+                    w3_q[b] = late[:, b * N : (b + 1) * N]
                 for c in range(2):
-                    scale_tile(i - 2, c, False)
-            if i < TILES:
-                look_tile(i)
-            side_work(i)
-            if i >= 1:
-                weigh_tile(i - 1)
-                if i + 1 < TILES:
-                    load_tpl(i + 1)
-                fill_tile(i - 1)
-        order = [(c, n) for c in range(2) for n in range(N_TILES)]
-        banks = [4, 5, 6, 7, 0, 1, 2, 3]
+                    f_q[0, c] = late[:, 2 * N + c * HALF : 2 * N + (c + 1) * HALF]
+                quantise_w3(0)
+                quantise_w3(1)
+            if k == TILES - 2:
+                for c in range(2):
+                    quantise_f(0, c, whole)
+
+        read_typed(0)
+        quantise_w1(0, 0)
+        quantise_w1(0, 1)
+        nc.scalar.activation(out=neg_temp[:], in_=temp_sb[:], func=ACT.Copy, scale=-1.0)
+        for k in range(-2, TILES):
+            if k + 2 < TILES:
+                read_tile(k + 2)
+            if k >= 0:
+                weigh_tile(k)
+                fill_tile(k)
+            if k + 2 < TILES:
+                centre_tile(k + 2)
+            if k + 3 < TILES:
+                read_typed(k + 3)
+            if 0 <= k + 1 < TILES:
+                look_tile(k + 1)
+            if 0 <= k < TILES - 1:
+                for c in range(2):
+                    scale_tile(k, c, whole, False)
+            side_work(k)
         for k in range(8):
-            open_sum(*order[k], banks[k])
-        scale_tile(TILES - 1, 0, True)
-        scale_tile(TILES - 1, 1, False)
+            open_sum(k)
+        for c in range(2):
+            f_q[1, c] = held([P, HALF], U32, "f_q1_%d" % c)[:]
+        last = TILES - 1
         for u in range(2):
-            quantise_f(1, 0, u, True)
+            scale_tile(last, 0, quarters[u], u == 0)
+            group_f(1, 0, u, u == 0)
+            quantise_f(1, 0, quarters[u])
+        scale_tile(last, 1, whole, False)
         for u in range(2):
-            quantise_f(1, 1, u, False)
-        for k in range(len(order)):
-            close_sum(*order[k], k % 2 == 0)
-            if k + 8 < len(order):
-                open_sum(*order[k + 8], banks[k])
+            group_f(1, 1, u, True)
+        quantise_f(1, 1, whole)
+        for k in range(len(parts)):
+            close_sum(k, k >= 5 and k % 2 == 1)
+            if k + 8 < len(parts):
+                open_sum(k + 8)

@@ -23,7 +23,7 @@ PASSES = H // (P * PACK)
 TILES = PASSES * PACK
 N_TILES = N // P
 W3_CHUNK = 256
-SIDE = {0:(0,1),1:(2,3),2:(4,5),3:(6,7),4:(8,9)}
+SIDE = {1:(0,),2:(1,3),3:(4,6),4:(7,8),5:(9,2),6:(5,)}
 
 
 def tile_list_placeholder_fill_kernel(tc, tab_words, tab_scales, offs, pos1, pos2, w1, w4_words, w4_scales,
@@ -65,7 +65,8 @@ def tile_list_placeholder_fill_kernel(tc, tab_words, tab_scales, offs, pos1, pos
         w1_raw = [held([P, PACK, HALF], F32, "w1_raw%d" % b) for b in range(PASSES)]
         w3_raw = [held([P, PACK, N], F32, "w3_raw%d" % b) for b in range(PASSES)]
         tpl_sb = [shared([P, NP], F32, "tpl%d" % i, "small%d" % i, 1) for i in range(TILES)]
-        wgs_sb = held([P, PACK, NP], F32, "wgs_sb")
+        wgs_first = held([P, 1, NP], F32, "wgs_first")
+        wgs_rest = held([P, PACK - 1, NP], F32, "wgs_rest")
 
         nc.vector.memset(tab_s[:].bitcast(I32), 0)
         nc.gpsimd.memset(w4_sraw[:].bitcast(I32), 0)
@@ -90,14 +91,17 @@ def tile_list_placeholder_fill_kernel(tc, tab_words, tab_scales, offs, pos1, pos
         bias_sb = load_row_values(nc.sync, bias, "bias_sb")
         temp_sb = load_row_values(nc.sync, temp, "temp_sb")
         mid_sb = load_row_values(nc.sync, mid, "mid_sb")
-        load_w1(1)
         nc.sync.dma_start(pos1_sb[:], pos1)
         load_tpl(0)
+        wgs_rows = wgs.rearrange("(q t) m -> q t m", t=PACK)
         for q in (0, 2, 1, 3):
-            nc.sync.dma_start(out=wgs_sb[32 * q : 32 * q + 32, :, :], in_=wgs.rearrange("(q t) m -> q t m", t=PACK))
+            nc.sync.dma_start(out=wgs_first[32 * q : 32 * q + 32, :, :], in_=wgs_rows[:, :1, :])
         nc.sync.dma_start(pos2_sb[:], pos2)
         gain_sb = load_row_values(nc.sync, gain, "gain_sb")
         load_tpl(1)
+        for q in (0, 2, 1, 3):
+            nc.sync.dma_start(out=wgs_rest[32 * q : 32 * q + 32, :, :], in_=wgs_rows[:, 1:, :])
+        load_w1(1)
         load_tpl(2)
         load_tpl(3)
         load_w3(0)
@@ -136,7 +140,7 @@ def tile_list_placeholder_fill_kernel(tc, tab_words, tab_scales, offs, pos1, pos
         def quantise_w1(b, u):
             first = 1 - b
             if u == 0:
-                w1_g[b] = ring([P, PACK, P, PACK], BF16, "w1_g", 1)
+                w1_g[b] = shared([P, PACK, P, PACK], BF16, "w1_g", "h", 3)
             nc.scalar.copy(out=w1_g[b][:, first:, 64 * u : 64 * (u + 1), :].rearrange("p t m j -> p m j t"),
                            in_=w1_raw[b][:, :, 256 * u : 256 * (u + 1)].rearrange("p j (m t) -> p m j t", t=PACK)[:, :, :, first:])
             if u == 1:
@@ -147,24 +151,25 @@ def tile_list_placeholder_fill_kernel(tc, tab_words, tab_scales, offs, pos1, pos
         page_top = held([P, TILES], F32, "page_top")
         look_bias = held([P, TILES], F32, "look_bias")
 
-        w3_s = [held([P, N], U8, "w3_s%d" % b) for b in range(PASSES)]
-        w3_g, w3_q, f_q, f_g = {}, {}, {}, {}
+        w3_g, w3_q, w3_s, f_q, f_s, f_g = {}, {}, {}, {}, {}, {}
 
         def group_w3(b, u):
-            if u == 0:
-                w3_g[b] = held([P, N, PACK], BF16, "w3_g%d" % b)
-            cols = slice(u * W3_CHUNK, (u + 1) * W3_CHUNK)
-            nc.scalar.copy(out=w3_g[b][:, cols, :].rearrange("p (c i) t -> p c t i", i=4),
-                           in_=w3_raw[b][:, :, cols].rearrange("p t (c i) -> p c t i", i=4))
+            part, first = divmod(u, 2)
+            if first == 0:
+                w3_g[b, part] = held([P, min(HALF, N - part * HALF), PACK], BF16, "w3_g%d_%d" % (b, part))
+            dst = w3_g[b, part][:, first * W3_CHUNK : (first + 1) * W3_CHUNK, :]
+            nc.scalar.copy(out=dst.rearrange("p (c i) t -> p c t i", i=4),
+                           in_=w3_raw[b][:, :, u * W3_CHUNK : (u + 1) * W3_CHUNK].rearrange("p t (c i) -> p c t i", i=4))
 
-        def quantise_w3(b):
-            for u in range(2):
-                cols = slice(u * N // 2, (u + 1) * N // 2)
-                nc.vector.quantize_mx(out=w3_q[b][:, cols].bitcast(FP8X4), scales=w3_s[b][:, cols],
-                                      in_=w3_g[b][:, cols, :].rearrange("p c t -> p (c t)"))
+        def quantise_w3(b, part, codes):
+            width = min(HALF, N - part * HALF)
+            plane = held([P, width], U8, "w3_s%d_%d" % (b, part))
+            nc.vector.quantize_mx(out=codes.bitcast(FP8X4), scales=plane[:], in_=w3_g[b, part][:].rearrange("p c t -> p (c t)"))
+            for a in range(width // P):
+                w3_q[b, PACK * part + a] = codes[:, a * P : (a + 1) * P]
+                w3_s[b, PACK * part + a] = plane[:, a * P : (a + 1) * P]
 
-        scaled = [[held([P, PACK, HALF], BF16, "scaled%d_%d" % (b, c)) for c in range(2)] for b in range(PASSES)]
-        f_s = [[held([P, HALF], U8, "f_s%d_%d" % (b, c)) for c in range(2)] for b in range(PASSES)]
+        scaled = [[ring([P, PACK, HALF], BF16, "scaled%d_%d" % (b, c), 1) for c in range(2)] for b in range(PASSES)]
         pages, looks, weights = {}, {}, {}
 
         readings = {}
@@ -200,13 +205,14 @@ def tile_list_placeholder_fill_kernel(tc, tab_words, tab_scales, offs, pos1, pos
 
         def look_tile(i):
             col = slice(i, i + 1)
-            looks[i] = ring([P, NP], F32, "look", 3)
+            tag, bufs = {2: ("early6", 1), 3: ("early7", 1)}.get(i, ("look", 3))
+            looks[i] = shared([P, NP], F32, "look", tag, bufs)
             nc.scalar.activation(out=looks[i][:], in_=readings[i][:].indirect(pos1_sb[:]), func=ACT.Exp,
                                  bias=look_bias[:, col], scale=temp_sb[:, col])
 
         def weigh_tile(i):
-            weights[i] = shared([P, NP], F32, "weight", "late", 1) if i == TILES - 3 else ring([P, NP], F32, "weight", 2)
-            nc.gpsimd.tensor_tensor(weights[i][:], tpl_sb[i][:], wgs_sb[:, i % PACK, :], ALU.mult)
+            weights[i] = shared([P, NP], F32, "weight", "weight" if i < TILES - 2 else "early%d" % i, 1)
+            nc.gpsimd.tensor_tensor(weights[i][:], tpl_sb[i][:], wgs_first[:, 0, :] if i % PACK == 0 else wgs_rest[:, i % PACK - 1, :], ALU.mult)
 
         def fill_tile(i):
             nc.vector.tensor_tensor(pages[i][:].indirect(pos2_sb[:]), looks[i][:], weights[i][:], ALU.mult)
@@ -222,43 +228,46 @@ def tile_list_placeholder_fill_kernel(tc, tab_words, tab_scales, offs, pos1, pos
         quarters = [slice(0, 256), slice(256, 512)]
         whole = slice(0, HALF)
 
-        def group_f(b, c, u, on_vector):
-            if u == 0:
-                f_g[b, c] = ring([P, HALF, PACK], BF16, "f_g", 3)
-            dst = f_g[b, c][:, quarters[u], :].rearrange("p (c i) t -> p c t i", i=4)
+        def group_f(dst, b, c, u, on_vector):
+            dst = dst.rearrange("p (c i) t -> p c t i", i=4)
             src = scaled[b][c][:, :, quarters[u]].rearrange("p t (c i) -> p c t i", i=4)
             if on_vector:
                 nc.vector.tensor_copy(out=dst, in_=src)
             else:
                 nc.scalar.copy(out=dst, in_=src)
 
-        def quantise_f(b, c, cols):
-            nc.vector.quantize_mx(out=f_q[b, c][:, cols].bitcast(FP8X4), scales=f_s[b][c][:, cols],
-                                  in_=f_g[b, c][:, cols, :].rearrange("p c t -> p (c t)"))
+        def quantise_f(grouped, codes, name):
+            plane = held([P, codes.shape[1]], U8, name)
+            nc.vector.quantize_mx(out=codes.bitcast(FP8X4), scales=plane[:], in_=grouped.rearrange("p c t -> p (c t)"))
+            return codes, plane[:]
 
-        parts = [(0, quarters[u], (n, n + 1)) for u in range(2) for n in range(0, N_TILES, 2)]
-        parts = parts + [(1, whole, (n,)) for n in range(N_TILES)]
+        parts = []
+        for rows in (range(0, 4), range(4, N_TILES)):
+            parts = parts + [(0, u, (n, n + 1)) for u in range(2) for n in rows[::2]]
+            parts = parts + [(1, None, (n,)) for n in rows]
         banks = [4, 5, 6, 7, 0, 1, 2, 3]
         sums = {}
 
-        def add_pass(k, w_q, w_s, x_q, x_s, start, stop):
-            c, cols, rows = parts[k]
-            width = cols.stop - cols.start
+        def add_pass(k, weight_of, x_q, x_s, start, stop):
+            rows = parts[k][2]
+            width = HALF // len(rows)
             for a, n in enumerate(rows):
-                w_cols = slice(n * P, (n + 1) * P)
-                nc.tensor.matmul_mx(out=sums[k][:, a * width : (a + 1) * width], lhsT=w_q[:, w_cols].bitcast(FP8X4),
-                                    lhsT_scale=w_s[:, w_cols], rhs=x_q[:, cols].bitcast(FP8X4), rhs_scale=x_s[:, cols],
+                w_q, w_s = weight_of(n)
+                nc.tensor.matmul_mx(out=sums[k][:, a * width : (a + 1) * width], lhsT=w_q.bitcast(FP8X4), lhsT_scale=w_s,
+                                    rhs=x_q.bitcast(FP8X4), rhs_scale=x_s,
                                     start=start and a == 0, stop=stop and a == len(rows) - 1)
 
         def open_sum(k):
-            c = parts[k][0]
+            c, u, rows = parts[k]
+            cols = whole if u is None else quarters[u]
             sums[k] = psum.tile([P, HALF], F32, name="acc", tag="bank%d" % banks[k % 8])
-            add_pass(k, w6_q, w6_s, v_q[c], v_s[c], True, False)
-            add_pass(k, w3_q[0], w3_s[0], f_q[0, c], f_s[0][c], False, False)
+            add_pass(k, lambda n: (w6_q[:, n * P : (n + 1) * P], w6_s[:, n * P : (n + 1) * P]), v_q[c][:, cols], v_s[c][:, cols], True, False)
+            add_pass(k, lambda n: (w3_q[0, n], w3_s[0, n]), f_early[c][0][:, cols], f_early[c][1][:, cols], False, False)
 
         def close_sum(k, on_vector):
-            c, cols, rows = parts[k]
-            add_pass(k, w3_q[1], w3_s[1], f_q[1, c], f_s[1][c], False, True)
+            c, u, rows = parts[k]
+            cols = whole if u is None else quarters[u]
+            add_pass(k, lambda n: (w3_q[1, n], w3_s[1, n]), f_last[c, u][0], f_last[c, u][1], False, True)
             result = shared([P, HALF], F32, "result", "small%d" % k, 1)
             if on_vector:
                 nc.vector.tensor_copy(out=result[:], in_=sums[k][:])
@@ -268,26 +277,26 @@ def tile_list_placeholder_fill_kernel(tc, tab_words, tab_scales, offs, pos1, pos
             nc.sync.dma_start(out=dst.rearrange("(a p) j -> p a j", p=P), in_=result[:].rearrange("p (a j) -> p a j", a=len(rows)))
 
         def side_work(k):
-            if k == -1:
+            if k == 0:
                 quantise_w1(1, 0)
                 quantise_w1(1, 1)
             for job in SIDE.get(k, ()):
                 if job < 6:
                     group_w3(job // 3, job % 3)
                 else:
-                    group_f(0, (job - 6) // 2, job % 2, False)
+                    c, u = divmod(job - 6, 2)
+                    if u == 0:
+                        f_g[c] = held([P, HALF, PACK], BF16, "f_g%d" % c)
+                    group_f(f_g[c][:, quarters[u], :], 0, c, u, False)
             if k == TILES - 3:
-                late = shared([P, 2 * N + S], U32, "late", "late", 1)
-                for b in range(PASSES):
-                    w3_q[b] = late[:, b * N : (b + 1) * N]
-                for c in range(2):
-                    f_q[0, c] = late[:, 2 * N + c * HALF : 2 * N + (c + 1) * HALF]
-                quantise_w3(0)
-                quantise_w3(1)
+                late[0] = shared([P, 2 * S], U32, "late", "weight", 1)
+                quantise_w3(0, 0, late[0][:, :HALF])
             if k == TILES - 2:
                 for c in range(2):
-                    quantise_f(0, c, whole)
+                    f_early[c] = quantise_f(f_g[c][:], late[0][:, (1 + c) * HALF : (2 + c) * HALF], "f_s%d" % c)
+                quantise_w3(1, 0, late[0][:, 3 * HALF :])
 
+        late, f_early, f_last = {}, {}, {}
         read_typed(0)
         quantise_w1(0, 0)
         quantise_w1(0, 1)
@@ -310,18 +319,22 @@ def tile_list_placeholder_fill_kernel(tc, tab_words, tab_scales, offs, pos1, pos
             side_work(k)
         for k in range(8):
             open_sum(k)
-        for c in range(2):
-            f_q[1, c] = held([P, HALF], U32, "f_q1_%d" % c)[:]
         last = TILES - 1
         for u in range(2):
-            scale_tile(last, 0, quarters[u], u == 0)
-            group_f(1, 0, u, u == 0)
-            quantise_f(1, 0, quarters[u])
+            scale_tile(last, 0, quarters[u], True)
         scale_tile(last, 1, whole, False)
+        narrow = [held([P, W3_CHUNK, PACK], BF16, "f_g_narrow%d" % u) for u in range(2)]
+        wide = held([P, HALF, PACK], BF16, "f_g_wide")
         for u in range(2):
-            group_f(1, 1, u, True)
-        quantise_f(1, 1, whole)
+            group_f(narrow[u][:], 1, 0, u, True)
+        for u in range(2):
+            f_last[0, u] = quantise_f(narrow[u][:], held([P, W3_CHUNK], U32, "f_q_narrow%d" % u)[:], "f_s_narrow%d" % u)
+        for u in range(2):
+            group_f(wide[:, quarters[u], :], 1, 1, u, u == 1)
+        f_last[1, None] = quantise_f(wide[:], held([P, HALF], U32, "f_q_wide")[:], "f_s_wide")
+        for b in range(PASSES):
+            quantise_w3(b, 1, shared([P, W3_CHUNK], U32, "latest", "scaled1_%d" % b, 1)[:])
         for k in range(len(parts)):
+            if k >= 8:
+                open_sum(k)
             close_sum(k, k >= 5 and k % 2 == 1)
-            if k + 8 < len(parts):
-                open_sum(k + 8)

@@ -261,8 +261,10 @@ def tile_list_placeholder_fill_kernel(tc, tab_words, tab_scales, offs, pos1, pos
             c, u, rows = parts[k]
             cols = whole if u is None else quarters[u]
             sums[k] = psum.tile([P, HALF], F32, name="acc", tag="bank%d" % banks[k % 8])
-            add_pass(k, lambda n: (w6_q[:, n * P : (n + 1) * P], w6_s[:, n * P : (n + 1) * P]), v_q[c][:, cols], v_s[c][:, cols], True, False)
-            add_pass(k, lambda n: (w3_q[0, n], w3_s[0, n]), f_early[c][0][:, cols], f_early[c][1][:, cols], False, False)
+            tokens = (lambda n: (w6_q[:, n * P : (n + 1) * P], w6_s[:, n * P : (n + 1) * P]), v_q[c][:, cols], v_s[c][:, cols])
+            early = (lambda n: (w3_q[0, n], w3_s[0, n]), f_early[c][0][:, cols], f_early[c][1][:, cols])
+            for a, operands in enumerate((early, tokens) if k < 8 else (tokens, early)):
+                add_pass(k, *operands, a == 0, False)
 
         def close_sum(k, on_vector):
             c, u, rows = parts[k]
@@ -289,12 +291,12 @@ def tile_list_placeholder_fill_kernel(tc, tab_words, tab_scales, offs, pos1, pos
                         f_g[c] = held([P, HALF, PACK], BF16, "f_g%d" % c)
                     group_f(f_g[c][:, quarters[u], :], 0, c, u, False)
             if k == TILES - 3:
-                late[0] = shared([P, 2 * S], U32, "late", "weight", 1)
-                quantise_w3(0, 0, late[0][:, :HALF])
+                late[0] = shared([P, 3 * HALF], U32, "late", "weight", 1)
+                quantise_w3(1, 0, late[0][:, :HALF])
             if k == TILES - 2:
                 for c in range(2):
                     f_early[c] = quantise_f(f_g[c][:], late[0][:, (1 + c) * HALF : (2 + c) * HALF], "f_s%d" % c)
-                quantise_w3(1, 0, late[0][:, 3 * HALF :])
+                quantise_w3(0, 0, shared([P, HALF], U32, "later", "early6", 1)[:])
 
         late, f_early, f_last = {}, {}, {}
         read_typed(0)

from contextlib import ExitStack

import concourse.mybir as mybir

K, T, S, NP, H, N = 512, 4096, 1024, 512, 1024, 768
FLOPS = 2 * S * (2 * K * H + H * N + K * N)

F32 = mybir.dt.float32
BF16 = mybir.dt.bfloat16
I32 = mybir.dt.int32
U32 = mybir.dt.uint32
U16 = mybir.dt.uint16
U8 = mybir.dt.uint8
FP8X4 = mybir.dt.float8_e4m3fn_x4
FP4X4 = mybir.dt.float4_e2m1fn_x4
ALU = mybir.AluOpType
ACT = mybir.ActivationFunctionType

P = 128
PACK = 4
HALF = 512
PASSES = H // (P * PACK)
TILES = PASSES * PACK
N_TILES = N // P
W3_CHUNK = 256
SIDE = {1:(0,),2:(1,3),3:(4,6),4:(7,8),5:(9,2),6:(5,)}


def tile_list_placeholder_fill_kernel(tc, tab_words, tab_scales, offs, pos1, pos2, w1, w4_words, w4_scales,
                                                bias, temp, tpl, mid, wgs, gain, w3, w6_words, w6_scales, out):
    nc = tc.nc
    with ExitStack() as ctx:
        keep = ctx.enter_context(tc.tile_pool(name="keep", bufs=1))
        work = ctx.enter_context(tc.tile_pool(name="work", bufs=1))
        psum = ctx.enter_context(tc.psum_pool(name="psum", bufs=1))

        def held(shape, dtype, name):
            return keep.tile(shape, dtype, name=name, align_bytes=64)

        def ring(shape, dtype, name, bufs):
            return work.tile(shape, dtype, name=name, tag=name, bufs=bufs, align_bytes=64)

        def shared(shape, dtype, name, tag, bufs):
            return work.tile(shape, dtype, name=name, tag=tag, bufs=bufs, align_bytes=64)

        def load_scale_rows(queue, plane, rows):
            for r in range(4):
                queue.dma_start(out=plane[r:P:32, :].bitcast(I32), in_=rows[0, r:16:4, :].bitcast(I32))

        def load_row_values(queue, vec, name):
            tile = held([P, TILES], F32, name)
            queue.dma_start(out=tile[:].rearrange("p (b t) -> p b t", t=PACK),
                            in_=vec.rearrange("(b p t) -> p b t", b=PASSES, t=PACK))
            return tile

        offs_sb = keep.tile([P, S // 16], U16, name="offs_sb")
        pos1_sb = keep.tile([P, NP // 16], U16, name="pos1_sb")
        pos2_sb = keep.tile([P, NP // 16], U16, name="pos2_sb")
        tab_w = held([P, T], U32, "tab_w")
        tab_s = held([P, T], U8, "tab_s")
        w4_raw = held([P, 2 * H], U8, "w4_raw")
        w4_sraw = held([P, H], U8, "w4_sraw")
        w6_q = held([P, N], U32, "w6_q")
        w6_s = held([P, N], U8, "w6_s")
        w1_raw = [held([P, PACK, HALF], F32, "w1_raw%d" % b) for b in range(PASSES)]
        w3_raw = [held([P, PACK, N], F32, "w3_raw%d" % b) for b in range(PASSES)]
        tpl_sb = [shared([P, NP], F32, "tpl%d" % i, "small%d" % i, 1) for i in range(TILES)]
        wgs_first = held([P, 1, NP], F32, "wgs_first")
        wgs_rest = held([P, PACK - 1, NP], F32, "wgs_rest")

        nc.vector.memset(tab_s[:].bitcast(I32), 0)
        nc.gpsimd.memset(w4_sraw[:].bitcast(I32), 0)
        nc.vector.memset(w6_s[:].bitcast(I32), 0)

        def load_w1(b):
            nc.sync.dma_start(out=w1_raw[b][:], in_=w1[:, b * HALF : (b + 1) * HALF].rearrange("(p j) c -> p j c", j=PACK))

        def load_tpl(i):
            b, t = divmod(i, PACK)
            nc.sync.dma_start(out=tpl_sb[i][:], in_=tpl[b * 512 : (b + 1) * 512, :].rearrange("(p t) m -> p t m", t=PACK)[:, t, :])

        def load_w3(b):
            nc.sync.dma_start(out=w3_raw[b][:], in_=w3[b * 512 : (b + 1) * 512, :].rearrange("(p t) n -> p t n", t=PACK))

        nc.sync.dma_start(offs_sb[:], offs)
        nc.sync.dma_start(out=tab_w[:].bitcast(I32), in_=tab_words[0].rearrange("p t i -> p (t i)").bitcast(I32))
        load_scale_rows(nc.sync, tab_s, tab_scales)
        nc.sync.dma_start(out=w4_raw[:].bitcast(I32), in_=w4_words[0].bitcast(I32))
        load_w1(0)
        load_scale_rows(nc.gpsimd, w4_sraw, w4_scales)
        bias_sb = load_row_values(nc.sync, bias, "bias_sb")
        temp_sb = load_row_values(nc.sync, temp, "temp_sb")
        mid_sb = load_row_values(nc.sync, mid, "mid_sb")
        nc.sync.dma_start(pos1_sb[:], pos1)
        load_tpl(0)
        wgs_rows = wgs.rearrange("(q t) m -> q t m", t=PACK)
        for q in (0, 2, 1, 3):
            nc.sync.dma_start(out=wgs_first[32 * q : 32 * q + 32, :, :], in_=wgs_rows[:, :1, :])
        nc.sync.dma_start(pos2_sb[:], pos2)
        gain_sb = load_row_values(nc.sync, gain, "gain_sb")
        load_tpl(1)
        for q in (0, 2, 1, 3):
            nc.sync.dma_start(out=wgs_rest[32 * q : 32 * q + 32, :, :], in_=wgs_rows[:, 1:, :])
        load_w1(1)
        load_tpl(2)
        load_tpl(3)
        load_w3(0)
        for i in range(PACK, TILES):
            load_tpl(i)
        load_w3(1)
        nc.sync.dma_start(out=w6_q[:].bitcast(I32), in_=w6_words[0].rearrange("p c i -> p (c i)").bitcast(I32))
        load_scale_rows(nc.sync, w6_s, w6_scales)

        v_q = [held([P, HALF], U32, "v_q%d" % c) for c in range(2)]
        v_s = [held([P, HALF], U8, "v_s%d" % c) for c in range(2)]
        for c in range(2):
            nc.vector.tensor_copy(v_q[c][:], tab_w[:].indirect(offs_sb[:, 32 * c : 32 * (c + 1)]))
        for c in range(2):
            nc.vector.tensor_copy(v_s[c][:], tab_s[:].indirect(offs_sb[:, 32 * c : 32 * (c + 1)]))

        w4_q = held([P, 2 * H], U8, "w4_q")
        w4_s = held([P, H], U8, "w4_s")
        nc.scalar.copy(out=w4_q[:].bitcast(U16).rearrange("p (b t m) -> p b m t", b=PASSES, t=PACK),
                       in_=w4_raw[:].bitcast(U16).rearrange("p (b m t) -> p b m t", b=PASSES, t=PACK))
        for b in range(PASSES):
            cols = slice(b * HALF, (b + 1) * HALF)
            nc.gpsimd.tensor_copy(out=w4_s[:, cols].rearrange("p (t m) -> p t m", t=PACK),
                                  in_=w4_sraw[:, cols].rearrange("p (m t) -> p t m", t=PACK))

        w1_q = [held([P, HALF], U32, "w1_q%d" % b) for b in range(PASSES)]
        w1_s = [held([P, HALF], U8, "w1_s%d" % b) for b in range(PASSES)]
        w1_g = {}

        w1_one = held([P, P, PACK], BF16, "w1_one")
        w1_first = w1_raw[0][:].rearrange("p j (m t) -> p t m j", t=PACK)[:, 0, :, :]
        nc.scalar.copy(out=w1_one[:, : P // 2, :], in_=w1_first[:, : P // 2, :])
        nc.vector.tensor_copy(out=w1_one[:, P // 2 :, :], in_=w1_first[:, P // 2 :, :])
        nc.vector.quantize_mx(out=w1_q[0][:, :P].bitcast(FP8X4), scales=w1_s[0][:, :P], in_=w1_one[:].rearrange("p m j -> p (m j)"))

        def quantise_w1(b, u):
            first = 1 - b
            if u == 0:
                w1_g[b] = shared([P, PACK, P, PACK], BF16, "w1_g", "h", 3)
            nc.scalar.copy(out=w1_g[b][:, first:, 64 * u : 64 * (u + 1), :].rearrange("p t m j -> p m j t"),
                           in_=w1_raw[b][:, :, 256 * u : 256 * (u + 1)].rearrange("p j (m t) -> p m j t", t=PACK)[:, :, :, first:])
            if u == 1:
                nc.vector.quantize_mx(out=w1_q[b][:, first * P :].bitcast(FP8X4), scales=w1_s[b][:, first * P :],
                                      in_=w1_g[b][:, first:, :, :].rearrange("p t m j -> p (t m j)"))

        neg_temp = held([P, TILES], F32, "neg_temp")
        page_top = held([P, TILES], F32, "page_top")
        look_bias = held([P, TILES], F32, "look_bias")

        w3_g, w3_q, w3_s, f_q, f_s, f_g = {}, {}, {}, {}, {}, {}

        def group_w3(b, u):
            part, first = divmod(u, 2)
            if first == 0:
                w3_g[b, part] = held([P, min(HALF, N - part * HALF), PACK], BF16, "w3_g%d_%d" % (b, part))
            dst = w3_g[b, part][:, first * W3_CHUNK : (first + 1) * W3_CHUNK, :]
            nc.scalar.copy(out=dst.rearrange("p (c i) t -> p c t i", i=4),
                           in_=w3_raw[b][:, :, u * W3_CHUNK : (u + 1) * W3_CHUNK].rearrange("p t (c i) -> p c t i", i=4))

        def quantise_w3(b, part, codes):
            width = min(HALF, N - part * HALF)
            plane = held([P, width], U8, "w3_s%d_%d" % (b, part))
            nc.vector.quantize_mx(out=codes.bitcast(FP8X4), scales=plane[:], in_=w3_g[b, part][:].rearrange("p c t -> p (c t)"))
            for a in range(width // P):
                w3_q[b, PACK * part + a] = codes[:, a * P : (a + 1) * P]
                w3_s[b, PACK * part + a] = plane[:, a * P : (a + 1) * P]

        scaled = [[ring([P, PACK, HALF], BF16, "scaled%d_%d" % (b, c), 1) for c in range(2)] for b in range(PASSES)]
        pages, looks, weights = {}, {}, {}

        readings = {}

        biased = {}

        def read_typed(i):
            for c in range(2):
                typed = psum.tile([P, HALF], F32, name="typed", tag="bank%d" % c)
                nc.tensor.matmul_mx(out=typed[:], lhsT=w4_q[:, 2 * P * i : 2 * P * (i + 1)].bitcast(FP4X4),
                                    lhsT_scale=w4_s[:, P * i : P * (i + 1)], rhs=v_q[c][:].bitcast(FP8X4),
                                    rhs_scale=v_s[c][:], start=True, stop=True)
                biased[i, c] = ring([P, HALF], F32, "biased", 4)
                nc.scalar.activation(out=biased[i, c][:], in_=typed[:], func=ACT.Identity, bias=bias_sb[:, i : i + 1])

        def read_tile(i):
            b, t = divmod(i, PACK)
            h = ring([P, S], F32, "h", 3)
            for c in range(2):
                plain = psum.tile([P, HALF], F32, name="plain", tag="bank%d" % (2 + c))
                nc.tensor.matmul_mx(out=plain[:], lhsT=w1_q[b][:, P * t : P * (t + 1)].bitcast(FP8X4),
                                    lhsT_scale=w1_s[b][:, P * t : P * (t + 1)], rhs=v_q[c][:].bitcast(FP8X4),
                                    rhs_scale=v_s[c][:], start=True, stop=True)
                nc.vector.tensor_tensor(h[:, c * HALF : (c + 1) * HALF], plain[:], biased[i, c][:], ALU.max)
            readings[i] = h

        def centre_tile(i):
            col = slice(i, i + 1)
            pages[i] = ring([P, S], F32, "page", 4)
            nc.vector.tensor_scalar(pages[i][:], readings[i][:], mid_sb[:, col], None, ALU.subtract, ALU.max,
                                    accum_out=page_top[:, col])
            nc.vector.tensor_scalar(look_bias[:, col], page_top[:, col], mid_sb[:, col], neg_temp[:, col], ALU.add, ALU.mult)

        def look_tile(i):
            col = slice(i, i + 1)
            tag, bufs = {2: ("early6", 1), 3: ("early7", 1)}.get(i, ("look", 3))
            looks[i] = shared([P, NP], F32, "look", tag, bufs)
            nc.scalar.activation(out=looks[i][:], in_=readings[i][:].indirect(pos1_sb[:]), func=ACT.Exp,
                                 bias=look_bias[:, col], scale=temp_sb[:, col])

        def weigh_tile(i):
            weights[i] = shared([P, NP], F32, "weight", "weight" if i < TILES - 2 else "early%d" % i, 1)
            nc.gpsimd.tensor_tensor(weights[i][:], tpl_sb[i][:], wgs_first[:, 0, :] if i % PACK == 0 else wgs_rest[:, i % PACK - 1, :], ALU.mult)

        def fill_tile(i):
            nc.vector.tensor_tensor(pages[i][:].indirect(pos2_sb[:]), looks[i][:], weights[i][:], ALU.mult)

        def scale_tile(i, c, cols, on_vector):
            b, t = divmod(i, PACK)
            src = pages[i][:, c * HALF : (c + 1) * HALF][:, cols]
            if on_vector:
                nc.vector.tensor_scalar(scaled[b][c][:, t, cols], src, gain_sb[:, i : i + 1], None, ALU.mult)
            else:
                nc.scalar.activation(out=scaled[b][c][:, t, cols], in_=src, func=ACT.Copy, scale=gain_sb[:, i : i + 1])

        quarters = [slice(0, 256), slice(256, 512)]
        whole = slice(0, HALF)

        def group_f(dst, b, c, u, on_vector):
            dst = dst.rearrange("p (c i) t -> p c t i", i=4)
            src = scaled[b][c][:, :, quarters[u]].rearrange("p t (c i) -> p c t i", i=4)
            if on_vector:
                nc.vector.tensor_copy(out=dst, in_=src)
            else:
                nc.scalar.copy(out=dst, in_=src)

        def quantise_f(grouped, codes, name):
            plane = held([P, codes.shape[1]], U8, name)
            nc.vector.quantize_mx(out=codes.bitcast(FP8X4), scales=plane[:], in_=grouped.rearrange("p c t -> p (c t)"))
            return codes, plane[:]

        parts = []
        for rows in (range(0, 4), range(4, N_TILES)):
            parts = parts + [(0, u, (n, n + 1)) for u in range(2) for n in rows[::2]]
            parts = parts + [(1, None, (n,)) for n in rows]
        banks = [4, 5, 6, 7, 0, 1, 2, 3]
        sums = {}

        def add_pass(k, weight_of, x_q, x_s, start, stop):
            rows = parts[k][2]
            width = HALF // len(rows)
            for a, n in enumerate(rows):
                w_q, w_s = weight_of(n)
                nc.tensor.matmul_mx(out=sums[k][:, a * width : (a + 1) * width], lhsT=w_q.bitcast(FP8X4), lhsT_scale=w_s,
                                    rhs=x_q.bitcast(FP8X4), rhs_scale=x_s,
                                    start=start and a == 0, stop=stop and a == len(rows) - 1)

        def open_sum(k):
            c, u, rows = parts[k]
            cols = whole if u is None else quarters[u]
            sums[k] = psum.tile([P, HALF], F32, name="acc", tag="bank%d" % banks[k % 8])
            tokens = (lambda n: (w6_q[:, n * P : (n + 1) * P], w6_s[:, n * P : (n + 1) * P]), v_q[c][:, cols], v_s[c][:, cols])
            early = (lambda n: (w3_q[0, n], w3_s[0, n]), f_early[c][0][:, cols], f_early[c][1][:, cols])
            for a, operands in enumerate((early, tokens) if k < 8 else (tokens, early)):
                add_pass(k, *operands, a == 0, False)

        def close_sum(k, on_vector):
            c, u, rows = parts[k]
            cols = whole if u is None else quarters[u]
            add_pass(k, lambda n: (w3_q[1, n], w3_s[1, n]), f_last[c, u][0], f_last[c, u][1], False, True)
            result = shared([P, HALF], F32, "result", "small%d" % k, 1)
            if on_vector:
                nc.vector.tensor_copy(out=result[:], in_=sums[k][:])
            else:
                nc.scalar.copy(out=result[:], in_=sums[k][:])
            dst = out[rows[0] * P : (rows[-1] + 1) * P, c * HALF + cols.start : c * HALF + cols.stop]
            nc.sync.dma_start(out=dst.rearrange("(a p) j -> p a j", p=P), in_=result[:].rearrange("p (a j) -> p a j", a=len(rows)))

        def side_work(k):
            if k == 0:
                quantise_w1(1, 0)
                quantise_w1(1, 1)
            for job in SIDE.get(k, ()):
                if job < 6:
                    group_w3(job // 3, job % 3)
                else:
                    c, u = divmod(job - 6, 2)
                    if u == 0:
                        f_g[c] = held([P, HALF, PACK], BF16, "f_g%d" % c)
                    group_f(f_g[c][:, quarters[u], :], 0, c, u, False)
            if k == TILES - 3:
                late[0] = shared([P, 3 * HALF], U32, "late", "weight", 1)
                quantise_w3(1, 0, late[0][:, :HALF])
            if k == TILES - 2:
                for c in range(2):
                    f_early[c] = quantise_f(f_g[c][:], late[0][:, (1 + c) * HALF : (2 + c) * HALF], "f_s%d" % c)
                quantise_w3(0, 0, shared([P, HALF], U32, "later", "early6", 1)[:])

        late, f_early, f_last = {}, {}, {}
        read_typed(0)
        quantise_w1(0, 0)
        quantise_w1(0, 1)
        nc.scalar.activation(out=neg_temp[:], in_=temp_sb[:], func=ACT.Copy, scale=-1.0)
        for k in range(-2, TILES):
            if k + 2 < TILES:
                read_tile(k + 2)
            if k >= 0:
                weigh_tile(k)
                fill_tile(k)
            if k + 2 < TILES:
                centre_tile(k + 2)
            if k + 3 < TILES:
                read_typed(k + 3)
            if 0 <= k + 1 < TILES:
                look_tile(k + 1)
            if 0 <= k < TILES - 1:
                for c in range(2):
                    scale_tile(k, c, whole, False)
            side_work(k)
        for k in range(8):
            open_sum(k)
        last = TILES - 1
        for u in range(2):
            scale_tile(last, 0, quarters[u], True)
        scale_tile(last, 1, whole, False)
        narrow = [held([P, W3_CHUNK, PACK], BF16, "f_g_narrow%d" % u) for u in range(2)]
        wide = held([P, HALF, PACK], BF16, "f_g_wide")
        for u in range(2):
            group_f(narrow[u][:], 1, 0, u, True)
        for u in range(2):
            f_last[0, u] = quantise_f(narrow[u][:], held([P, W3_CHUNK], U32, "f_q_narrow%d" % u)[:], "f_s_narrow%d" % u)
        for u in range(2):
            group_f(wide[:, quarters[u], :], 1, 1, u, u == 1)
        f_last[1, None] = quantise_f(wide[:], held([P, HALF], U32, "f_q_wide")[:], "f_s_wide")
        for b in range(PASSES):
            quantise_w3(b, 1, shared([P, W3_CHUNK], U32, "latest", "scaled1_%d" % b, 1)[:])
        for k in range(len(parts)):
            if k >= 8:
                open_sum(k)
            close_sum(k, k >= 5 and k % 2 == 1)
